import numpy as np
import ml_dtypes


def mxq(x, axis, fmt="e4m3"):
    dtype, down = {"e4m3": (ml_dtypes.float8_e4m3fn, 7), "e5m2": (ml_dtypes.float8_e5m2, 14)}[fmt]
    v = np.moveaxis(np.asarray(x, np.float32).astype(ml_dtypes.bfloat16).astype(np.float64), axis, -1)
    blocks = v.reshape(v.shape[:-1] + (-1, 32))
    amax = np.abs(blocks).max(-1, keepdims=True)
    byte = np.maximum(np.where(amax > 0, np.frexp(amax)[1] - 1 + 127, 0) - down, 1)
    scale = np.exp2(byte - 127.0)
    codes = (blocks / scale).astype(np.float32).astype(dtype).astype(np.float64)
    return np.moveaxis((codes * scale).reshape(v.shape), -1, axis)


WIDE = False


def mx_kscale(k):
    if not WIDE:
        return np.ones(k)
    levels = np.array([10, -10, 5, -5, 0])
    if k % 512:
        return np.exp2(np.random.permutation(np.resize(levels, k // 32))).repeat(32)
    a = np.empty((k // 512, 16))
    for p in range(k // 512):
        a[p, :8] = np.random.permutation(np.resize(levels, 8))
        for g in range(8):
            far = levels[np.abs(levels - a[p, g]) >= 10]
            a[p, g + 8] = far[np.random.randint(len(far))]
    return np.exp2(a.ravel()).repeat(32)


def f64(x):
    return np.asarray(x).astype(np.float64)


def striped(idx):
    return np.tile(idx.reshape(-1, 16).T, (8, 1)).astype(np.uint16)


def unstriped(offs):
    return offs[:16].T.reshape(-1).astype(np.int64)


E2M1 = np.array([0.0, 0.5, 1.0, 1.5, 2.0, 3.0, 4.0, 6.0, -0.0, -0.5, -1.0, -1.5, -2.0, -3.0, -4.0, -6.0])


def pack_weight(w, fmt):
    k, n = w.shape
    w = f64(np.asarray(w, np.float32).astype(ml_dtypes.bfloat16)).reshape(k // 32, 32, n)
    amax = np.abs(w).max(1)
    if fmt == "e4m3":
        byte = np.frexp(amax)[1] - 1 + 127 - 7
    else:
        mant, ex = np.frexp(amax / 6.0)
        byte = np.where(mant > 0.5, ex, ex - 1) + 127
    byte = np.clip(np.where(amax > 0, byte, 1), 1, 254)
    scaled = (w * np.exp2(127.0 - byte)[:, None, :]).reshape(k, n).astype(np.float32)
    by_word = np.ascontiguousarray(scaled.reshape(k // 512, 128, 4, n).transpose(0, 1, 3, 2))
    if fmt == "e4m3":
        words = by_word.astype(ml_dtypes.float8_e4m3fn).view(np.uint8)
    else:
        c = by_word.astype(ml_dtypes.float4_e2m1fn).view(np.uint8) & 0xF
        words = (c[..., 0::2] | (c[..., 1::2] << 4)).reshape(k // 512, 128, 2 * n)
    return np.ascontiguousarray(words), np.ascontiguousarray(byte.astype(np.uint8).reshape(k // 512, 16, n))


def unpack_weight(words, scales, fmt):
    g, _, n = scales.shape
    words = np.ascontiguousarray(words).reshape(g, 128, n, -1)
    if fmt == "e4m3":
        vals = words.view(ml_dtypes.float8_e4m3fn).astype(np.float64)
    else:
        nib = np.empty((g, 128, n, 4), np.uint8)
        nib[..., 0::2] = words & 0xF
        nib[..., 1::2] = words >> 4
        vals = E2M1[nib]
    vals = vals * np.repeat(np.exp2(scales.astype(np.float64) - 127.0), 8, axis=1)[..., None]
    return vals.transpose(0, 1, 3, 2).reshape(g * 512, n)


def gelu(v):
    return 0.5 * v * (1.0 + np.tanh(np.sqrt(2.0 / np.pi) * (v + 0.044715 * v**3)))


def striped8(idx):
    return np.concatenate([v.reshape(-1, 16).T for v in idx]).astype(np.uint16)


def unstriped8(offs):
    return np.stack([offs[16 * g:16 * g + 16].T.reshape(-1) for g in range(8)]).astype(np.int64)


def heads(h, wgt, idx8):
    r = np.arange(h.shape[0])
    return wgt[r // 4 % 128] * h[r[:, None], idx8[r % 512 // 64]]


def put_heads(h, wgs, idx8, t2):
    r = np.arange(h.shape[0])
    page = np.zeros((h.shape[0], t2))
    page[r[:, None], idx8[r % 512 // 64]] = wgs[r // 4 % 128] * h
    return page


K, T, S, P, T2, H, N = 1024, 2048, 1024, 1024, 2048, 512, 768


def setup_inputs():
    n = np.random.standard_normal
    s = mx_kscale(K)[:, None]
    u = mx_kscale(H)[:, None]
    d = {}
    d["tab_words"], d["tab_scales"] = pack_weight(n((K, T)) * s, "e4m3")
    d["offs"] = striped(np.random.permutation(T)[:S])
    d["offs2"] = striped8(np.stack([np.random.permutation(T2)[:S] for _ in range(8)]))
    d["offs3"] = striped8(np.stack([np.random.permutation(T2)[:P] for _ in range(8)]))
    d["w1"] = (n((K, H)) * (0.6 / K**0.5) / s * u.T).astype(np.float32)
    d["w2_words"], d["w2_scales"] = pack_weight(n((K, H)) * (0.6 / K**0.5) / s * u.T, "e2m1")
    d["soil"] = n((H, S)).astype(np.float32)
    d["wgs"] = np.repeat(np.random.uniform(0.5, 2.0, (8, S)), 16, axis=0).astype(np.float32)
    d["wgt"] = np.repeat(np.random.uniform(0.5, 2.0, (8, P)), 16, axis=0).astype(np.float32)
    d["frost"] = (n((H, P)) * u).astype(np.float32)
    d["w3"] = (n((H, N)) * (1.5 / H**0.5) / u).astype(np.float32)
    return d


def reference(tab_words, tab_scales, offs, offs2, offs3, w1, w2_words, w2_scales, soil, wgs, wgt, frost, w3):
    v = unpack_weight(tab_words, tab_scales, "e4m3")[:, unstriped(offs)]
    w2 = unpack_weight(w2_words, w2_scales, "e2m1")
    a = mxq(f64(w1), 0, "e4m3").T @ v
    b = w2.T @ v
    h = a * f64(soil) + b
    page = put_heads(h, f64(wgs), unstriped8(offs2), T2)
    x = heads(page, f64(wgt), unstriped8(offs3))
    f = f64(frost)
    capped = np.minimum(x, f)
    z = f - capped
    y = mxq(f64(w3), 0, "e4m3").T @ mxq(z, 0, "e4m3")
    return np.log(1.0 + np.abs(y))

@@ -1,0 +1,320 @@
+from contextlib import ExitStack
+
+import concourse.mybir as mybir
+
+K, T, S, PICKS, T2, H, N = 1024, 2048, 1024, 1024, 2048, 512, 768
+FLOPS = 2 * (2 * K * H * S + H * N * PICKS)
+
+F32 = mybir.dt.float32
+BF16 = mybir.dt.bfloat16
+I32 = mybir.dt.int32
+U32 = mybir.dt.uint32
+U16 = mybir.dt.uint16
+U8 = mybir.dt.uint8
+FP8X4 = mybir.dt.float8_e4m3fn_x4
+FP4X4 = mybir.dt.float4_e2m1fn_x4
+ALU = mybir.AluOpType
+ACT = mybir.ActivationFunctionType
+
+P = 128
+PACK = 4
+PASSES = K // (P * PACK)
+BANK = 512
+HALVES = S // BANK
+N_TILES = N // P
+CHUNKS = (256, 256, 256, 128, 128)
+MID = 31744
+RELU_ON_VECTOR = (0, 1, 2, 3, 4)
+
+
+def tile_list_needle_loss_plans_kernel(
+    tc, tab_words, tab_scales, offs, offs2, offs3, w1, w2_words, w2_scales, soil, wgs, wgt, frost, w3, out
+):
+    nc = tc.nc
+    with ExitStack() as ctx:
+        lists = ctx.enter_context(tc.tile_pool(name="lists", bufs=1))
+        keep = ctx.enter_context(tc.tile_pool(name="keep", bufs=1))
+        ring = ctx.enter_context(tc.tile_pool(name="ring", bufs=2))
+        arena = ctx.enter_context(tc.tile_pool(name="arena", bufs=1))
+        psum = ctx.enter_context(tc.psum_pool(name="psum", bufs=1))
+
+        def held(name, shape, dtype, tag=None):
+            return keep.tile(shape, dtype, name=name, tag=tag or name, align_bytes=64)
+
+        def placed(name, shape, dtype, offset):
+            return arena.tile(shape, dtype, name=name, align_bytes=64, offset=offset)
+
+        def bank(index):
+            return psum.tile([P, BANK], F32, name="bank%d" % (index % 8), tag="bank%d" % (index % 8))
+
+        pick = lists.tile([P, S // 16], U16, name="pick")
+        put = lists.tile([P, S // 16], U16, name="put")
+        read = lists.tile([P, PICKS // 16], U16, name="read")
+
+        tab_planes = held("tab_planes", [P, T], U8)
+        w2_planes_raw = held("w2_planes_raw", [P, PASSES, H], U8)
+        v_plane_low = held("v_plane_low", [P, S], U8)
+        pages = [held("page0", [P, T2], F32)]
+        nc.vector.memset(tab_planes[:].bitcast(U32), 0)
+        nc.gpsimd.memset(w2_planes_raw[:].rearrange("p a c -> p (a c)").bitcast(U32), 0)
+        nc.vector.memset(v_plane_low[:].bitcast(U32), 0)
+        for page in pages:
+            nc.vector.memset(page[:], 0.0)
+
+        tab = [placed("tab%d" % a, [P, T], U32, 4 * T * a) for a in range(PASSES)]
+        w1_raw = [held("w1_raw0", [P, PACK, H], F32), placed("w1_raw1", [P, PACK, H], F32, 8 * T)]
+        w2_raw = held("w2_raw", [P, PASSES, 2 * H], U8)
+        soil_rows = soil.rearrange("(p i) j -> i p j", i=PACK)
+        soil_sb = []
+
+        def load_tab(a):
+            nc.sync.dma_start(
+                out=tab[a][:].bitcast(I32), in_=tab_words[a].rearrange("p t i -> p (t i)").bitcast(I32)
+            )
+
+        def load_w1(a):
+            nc.sync.dma_start(
+                out=w1_raw[a][:], in_=w1[512 * a : 512 * (a + 1), :].rearrange("(p j) c -> p j c", j=PACK)
+            )
+
+        def load_soil(tile):
+            nc.sync.dma_start(out=tile[:], in_=soil_rows[len(soil_sb)])
+            soil_sb.append(tile)
+
+        nc.sync.dma_start(pick[:], offs)
+        load_tab(0)
+        load_tab(1)
+        nc.sync.dma_start(put[:], offs2)
+        for q in range(4):
+            nc.sync.dma_start(
+                out=tab_planes[32 * q : 32 * q + 4 * PASSES, :].bitcast(I32),
+                in_=tab_scales[:, 4 * q : 4 * q + 4, :].bitcast(I32),
+            )
+        for q in range(4):
+            nc.gpsimd.dma_start(
+                out=w2_planes_raw[32 * q : 32 * q + 4, :, :].bitcast(I32),
+                in_=w2_scales[:, 4 * q : 4 * q + 4, :].rearrange("a r c -> r a c").bitcast(I32),
+            )
+        nc.sync.dma_start(out=w2_raw[:].bitcast(I32), in_=w2_words.rearrange("a p c -> p a c").bitcast(I32))
+        load_w1(0)
+        load_w1(1)
+        load_soil(held("soil0", [P, S], F32))
+        nc.sync.dma_start(read[:], offs3)
+
+        v_words = [held("v_words%d" % a, [P, S], U32) for a in range(PASSES)]
+        nc.vector.tensor_copy(v_words[0][:], tab[0][:].indirect(pick[:]))
+        v_planes = placed("v_planes", [P, S], U8, 0)
+        nc.vector.tensor_copy(v_planes[:], tab_planes[:].indirect(pick[:]))
+        for q in range(4):
+            nc.sync.dma_start(
+                out=v_plane_low[32 * q : 32 * q + 4, :].bitcast(I32),
+                in_=v_planes[32 * q + 4 : 32 * q + 8, :].bitcast(I32),
+            )
+        wgs_sb = held("wgs_sb", [P, S], F32, tag="tab_planes")
+        nc.sync.dma_start(out=wgs_sb[:], in_=wgs)
+
+        w2_codes = held("w2_codes", [P, PASSES, 2 * H], U8)
+        w2_planes = placed("w2_planes", [P, PASSES, H], U8, S)
+        nc.scalar.copy(
+            out=w2_codes[:].bitcast(U16).rearrange("p a (i m) -> p a i m", i=PACK),
+            in_=w2_raw[:].bitcast(U16).rearrange("p a (m i) -> p a i m", i=PACK),
+        )
+        nc.vector.tensor_copy(
+            out=w2_planes[:].rearrange("p a (i m) -> p a i m", i=PACK),
+            in_=w2_planes_raw[:].rearrange("p a (m i) -> p a i m", i=PACK),
+        )
+
+        nc.vector.tensor_copy(v_words[1][:], tab[1][:].indirect(pick[:]))
+        load_soil(placed("soil1", [P, S], F32, 4 * T + 4 * S))
+
+        w1_codes = {}
+        w1_planes = {}
+
+        def quantise_w1(a, i0, i1, rounded):
+            count = i1 - i0
+            codes = held("w1_codes%d_%d" % (a, i0), [P, count * P], U32)
+            plane = held("w1_plane%d_%d" % (a, i0), [P, count * P], U8)
+            nc.scalar.copy(
+                out=rounded[:].rearrange("p i m j -> p m i j"),
+                in_=w1_raw[a][:].rearrange("p j (m i) -> p m i j", i=PACK)[:, :, i0:i1, :],
+            )
+            nc.vector.quantize_mx(
+                out=codes[:].bitcast(FP8X4), scales=plane[:], in_=rounded[:].rearrange("p i m j -> p (i m j)")
+            )
+            for i in range(i0, i1):
+                w1_codes[a, i] = codes[:, (i - i0) * P : (i - i0 + 1) * P]
+                w1_planes[a, i] = plane[:, (i - i0) * P : (i - i0 + 1) * P]
+
+        quantise_w1(0, 0, 1, held("w1_bf0", [P, 1, P, PACK], BF16))
+        quantise_w1(1, 0, 1, placed("w1_bf1", [P, 1, P, PACK], BF16, MID + 4096))
+
+        def products(i):
+            sums = []
+            for half in range(HALVES):
+                cols = slice(half * BANK, (half + 1) * BANK)
+                sums.append((cols, bank(4 * i + 2 * half), bank(4 * i + 2 * half + 1)))
+            for a in range(PASSES):
+                for cols, first, second in sums:
+                    nc.tensor.matmul_mx(
+                        out=second[:],
+                        lhsT=w2_codes[:, a, 2 * i * P : 2 * (i + 1) * P].bitcast(FP4X4),
+                        lhsT_scale=w2_planes[:, a, i * P : (i + 1) * P],
+                        rhs=v_words[a][:, cols].bitcast(FP8X4),
+                        rhs_scale=v_planes[:, cols] if a == 0 else v_plane_low[:, cols],
+                        start=(a == 0),
+                        stop=(a == PASSES - 1),
+                    )
+                for cols, first, second in sums:
+                    nc.tensor.matmul_mx(
+                        out=first[:],
+                        lhsT=w1_codes[a, i].bitcast(FP8X4),
+                        lhsT_scale=w1_planes[a, i],
+                        rhs=v_words[a][:, cols].bitcast(FP8X4),
+                        rhs_scale=v_planes[4 * a : P, cols],
+                        start=(a == 0),
+                        stop=(a == PASSES - 1),
+                    )
+            return sums
+
+        def weigh(i, h, sums):
+            for part, (cols, first, second) in zip(h, sums):
+                nc.vector.tensor_tensor(part, first[:], soil_sb[i][:, cols], ALU.mult)
+
+        def add(h, sums):
+            for part, (cols, first, second) in zip(h, sums):
+                nc.vector.tensor_tensor(part, second[:], part, ALU.add)
+
+        def halves(h):
+            return [h[:, half * BANK : (half + 1) * BANK] for half in range(HALVES)]
+
+        def scatter(i, h):
+            nc.vector.tensor_tensor(pages[i][:].indirect(put[:]), h[:], wgs_sb[:], ALU.mult)
+
+        def scatter_half(half, h):
+            nc.vector.tensor_tensor(
+                pages[0][:].indirect(put[:, half * BANK // 16 : (half + 1) * BANK // 16]),
+                h[:],
+                wgs_sb[:, half * BANK : (half + 1) * BANK],
+                ALU.mult,
+            )
+
+        w3_codes = held("w3_codes", [P, N], U32)
+        w3_plane = held("w3_plane", [P, N], U8)
+
+        def quantise_w3():
+            rounded = held("w3_bf", [P, N, PACK], BF16)
+            nc.scalar.copy(
+                out=rounded[:].rearrange("p (c k) j -> p c j k", k=4),
+                in_=w3_raw[:].rearrange("p j (c k) -> p c j k", k=4),
+            )
+            for n0, n1 in ((0, 512), (512, N)):
+                nc.vector.quantize_mx(
+                    out=w3_codes[:, n0:n1].bitcast(FP8X4),
+                    scales=w3_plane[:, n0:n1],
+                    in_=rounded[:, n0:n1, :].rearrange("p n j -> p (n j)"),
+                )
+
+        def late_page(page):
+            nc.gpsimd.memset(page[:], 0.0)
+            pages.append(page)
+
+        sums = products(0)
+        h = held("h0_first", [P, BANK], F32)
+        weigh(0, [h[:]], sums[:1])
+        add([h[:]], sums[:1])
+        scatter_half(0, h)
+        quantise_w1(1, 1, PACK, placed("w1_bf1_rest", [P, PACK - 1, P, PACK], BF16, MID))
+        load_soil(placed("soil2", [P, S], F32, 8 * T))
+        load_soil(placed("soil3", [P, S], F32, 8 * T + 4 * S))
+        quantise_w1(0, 1, PACK, placed("w1_bf0_rest", [P, PACK - 1, P, PACK], BF16, MID + 3072))
+        w3_raw = held("w3_raw", [P, PACK, N], F32, tag="w1_raw0")
+        nc.sync.dma_start(out=w3_raw[:], in_=w3.rearrange("(p j) n -> p j n", j=PACK))
+        late_page(placed("page1", [P, T2], F32, MID + 1024 - 4 * T2))
+        late_page(placed("page2", [P, T2], F32, MID + 5120))
+        h = placed("h0_second", [P, BANK], F32, MID + 2048)
+        weigh(0, [h[:]], sums[1:])
+        wgt_sb = held("wgt_sb", [P, PICKS], F32, tag="soil0")
+        nc.sync.dma_start(out=wgt_sb[:], in_=wgt)
+        add([h[:]], sums[1:])
+        scatter_half(1, h)
+        sums = products(1)
+        h = placed("h1", [P, S], F32, MID + 1024)
+        weigh(1, halves(h), sums)
+        late_page(placed("page3", [P, T2], F32, 4 * T))
+        add(halves(h), sums)
+        for i in range(1, PACK - 1):
+            sums = products(i + 1)
+            ahead = held("h2", [P, S], F32) if i == 1 else placed("h3", [P, S], F32, MID + 1024)
+            weigh(i + 1, halves(ahead), sums)
+            scatter(i, h)
+            add(halves(ahead), sums)
+            h = ahead
+        frost_sb = held("frost_sb", [P, PACK, PICKS], F32, tag="v_words0")
+        nc.sync.dma_start(out=frost_sb[:], in_=frost.rearrange("(p i) m -> p i m", i=PACK))
+        quantise_w3()
+        scatter(PACK - 1, h)
+
+        starts = [sum(CHUNKS[:c]) for c in range(len(CHUNKS))]
+        out_rows = out.rearrange("(t p) m -> p t m", p=P)
+        gap = {}
+        rounded_z = {}
+        banks_used = [0]
+
+        def gather(c, i):
+            m0, width = starts[c], CHUNKS[c]
+            if i == 0:
+                gap[c] = ring.tile([P, PACK, width], F32, name="gap")
+            nc.vector.tensor_tensor(
+                gap[c][:, i, :],
+                pages[i][:].indirect(read[:, m0 // 16 : (m0 + width) // 16]),
+                wgt_sb[:, m0 : m0 + width],
+                ALU.mult,
+            )
+
+        def subtract(c):
+            m0, width = starts[c], CHUNKS[c]
+            nc.vector.tensor_tensor(gap[c][:], frost_sb[:, :, m0 : m0 + width], gap[c][:], ALU.subtract)
+
+        def clip(c):
+            width = CHUNKS[c]
+            rounded_z[c] = held("z_bf%d" % c, [P, width, PACK], BF16)
+            dst = rounded_z[c][:].rearrange("p (g k) i -> p g i k", k=4)
+            src = gap[c][:].rearrange("p i (g k) -> p g i k", k=4)
+            if c in RELU_ON_VECTOR:
+                nc.vector.tensor_scalar_max(dst, src, 0.0)
+            else:
+                nc.scalar.activation(dst, src, ACT.Relu)
+
+        def finish(c):
+            m0, width = starts[c], CHUNKS[c]
+            codes = held("z_codes%d" % c, [P, width], U32)
+            plane = held("z_plane%d" % c, [P, width], U8)
+            nc.vector.quantize_mx(
+                out=codes[:].bitcast(FP8X4), scales=plane[:], in_=rounded_z[c][:].rearrange("p m i -> p (m i)")
+            )
+            per_bank = 2 if width == 256 else 3
+            for t0 in range(0, N_TILES, per_bank):
+                acc = bank(banks_used[0])
+                banks_used[0] = banks_used[0] + 1
+                for t in range(t0, t0 + per_bank):
+                    nc.tensor.matmul_mx(
+                        out=acc[:, (t - t0) * width : (t - t0 + 1) * width],
+                        lhsT=w3_codes[:, t * P : (t + 1) * P].bitcast(FP8X4),
+                        lhsT_scale=w3_plane[:, t * P : (t + 1) * P],
+                        rhs=codes[:].bitcast(FP8X4),
+                        rhs_scale=plane[:],
+                        start=True,
+                        stop=True,
+                    )
+                size = ring.tile([P, per_bank * width], F32, name="size", bufs=3)
+                result = ring.tile([P, per_bank, width], F32, name="result", bufs=4)
+                nc.scalar.activation(size[:], acc[:, : per_bank * width], ACT.Abs)
+                nc.scalar.activation(result[:].rearrange("p t m -> p (t m)"), size[:], ACT.Ln, bias=1.0)
+                nc.sync.dma_start(out=out_rows[:, t0 : t0 + per_bank, m0 : m0 + width], in_=result[:])
+
+        for c in range(len(CHUNKS)):
+            for i in range(PACK):
+                gather(c, i)
+            subtract(c)
+            clip(c)
+            finish(c)

@@ -22,9 +22,10 @@ PASSES = K // (P * PACK)
 BANK = 512
 HALVES = S // BANK
 N_TILES = N // P
-CHUNKS = (256, 256, 256, 128, 128)
-MID = 31744
-RELU_ON_VECTOR = (0, 1, 2, 3, 4)
+CHUNKS = (128, 256, 256, 128, 128, 128)
+GAP_SLOT = (0, 0, 1, 0, 1, 1)
+MID = 44032
+RELU_ON_VECTOR = (0, 1, 2, 3, 4, 5)
 
 
 def tile_list_needle_loss_plans_kernel(
@@ -51,7 +52,7 @@ def tile_list_needle_loss_plans_kernel(
         put = lists.tile([P, S // 16], U16, name="put")
         read = lists.tile([P, PICKS // 16], U16, name="read")
 
-        tab_planes = held("tab_planes", [P, T], U8)
+        tab_planes = placed("tab_planes", [P, T], U8, 60416)
         w2_planes_raw = held("w2_planes_raw", [P, PASSES, H], U8)
         v_plane_low = held("v_plane_low", [P, S], U8)
         pages = [held("page0", [P, T2], F32)]
@@ -59,11 +60,12 @@ def tile_list_needle_loss_plans_kernel(
         nc.gpsimd.memset(w2_planes_raw[:].rearrange("p a c -> p (a c)").bitcast(U32), 0)
         nc.vector.memset(v_plane_low[:].bitcast(U32), 0)
         for page in pages:
-            nc.vector.memset(page[:], 0.0)
+            nc.vector.memset(page[:, : T2 // 2 - 1], 0.0)
+            nc.vector.memset(page[:, T2 // 2 - 1 :], 0.0)
 
         tab = [placed("tab%d" % a, [P, T], U32, 4 * T * a) for a in range(PASSES)]
-        w1_raw = [held("w1_raw0", [P, PACK, H], F32), placed("w1_raw1", [P, PACK, H], F32, 8 * T)]
-        w2_raw = held("w2_raw", [P, PASSES, 2 * H], U8)
+        w1_raw = []
+        w2_raw = placed("w2_raw", [P, PASSES, 2 * H], U8, 12 * T - 2 * H)
         soil_rows = soil.rearrange("(p i) j -> i p j", i=PACK)
         soil_sb = []
 
@@ -73,6 +75,7 @@ def tile_list_needle_loss_plans_kernel(
             )
 
         def load_w1(a):
+            w1_raw.append(placed("w1_raw%d" % a, [P, PACK, H], F32, 12 * T - 4 * T * a))
             nc.sync.dma_start(
                 out=w1_raw[a][:], in_=w1[512 * a : 512 * (a + 1), :].rearrange("(p j) c -> p j c", j=PACK)
             )
@@ -82,9 +85,11 @@ def tile_list_needle_loss_plans_kernel(
             soil_sb.append(tile)
 
         nc.sync.dma_start(pick[:], offs)
+        nc.sync.dma_start(put[:], offs2)
+        nc.sync.dma_start(read[:], offs3)
+        nc.sync.dma_start(out=w2_raw[:].bitcast(I32), in_=w2_words.rearrange("a p c -> p a c").bitcast(I32))
         load_tab(0)
         load_tab(1)
-        nc.sync.dma_start(put[:], offs2)
         for q in range(4):
             nc.sync.dma_start(
                 out=tab_planes[32 * q : 32 * q + 4 * PASSES, :].bitcast(I32),
@@ -95,14 +100,18 @@ def tile_list_needle_loss_plans_kernel(
                 out=w2_planes_raw[32 * q : 32 * q + 4, :, :].bitcast(I32),
                 in_=w2_scales[:, 4 * q : 4 * q + 4, :].rearrange("a r c -> r a c").bitcast(I32),
             )
-        nc.sync.dma_start(out=w2_raw[:].bitcast(I32), in_=w2_words.rearrange("a p c -> p a c").bitcast(I32))
+
+        w2_codes = held("w2_codes", [P, PASSES, 2 * H], U8)
+        nc.scalar.copy(
+            out=w2_codes[:].bitcast(U16).rearrange("p a (i m) -> p a i m", i=PACK),
+            in_=w2_raw[:].bitcast(U16).rearrange("p a (m i) -> p a i m", i=PACK),
+        )
         load_w1(0)
         load_w1(1)
-        load_soil(held("soil0", [P, S], F32))
-        nc.sync.dma_start(read[:], offs3)
 
-        v_words = [held("v_words%d" % a, [P, S], U32) for a in range(PASSES)]
+        v_words = [held("v_words0", [P, S], U32)]
         nc.vector.tensor_copy(v_words[0][:], tab[0][:].indirect(pick[:]))
+        load_soil(placed("soil0", [P, S], F32, 4 * S))
         v_planes = placed("v_planes", [P, S], U8, 0)
         nc.vector.tensor_copy(v_planes[:], tab_planes[:].indirect(pick[:]))
         for q in range(4):
@@ -110,22 +119,17 @@ def tile_list_needle_loss_plans_kernel(
                 out=v_plane_low[32 * q : 32 * q + 4, :].bitcast(I32),
                 in_=v_planes[32 * q + 4 : 32 * q + 8, :].bitcast(I32),
             )
-        wgs_sb = held("wgs_sb", [P, S], F32, tag="tab_planes")
+        wgs_sb = placed("wgs_sb", [P, S], F32, 57344)
         nc.sync.dma_start(out=wgs_sb[:], in_=wgs)
 
-        w2_codes = held("w2_codes", [P, PASSES, 2 * H], U8)
-        w2_planes = placed("w2_planes", [P, PASSES, H], U8, S)
-        nc.scalar.copy(
-            out=w2_codes[:].bitcast(U16).rearrange("p a (i m) -> p a i m", i=PACK),
-            in_=w2_raw[:].bitcast(U16).rearrange("p a (m i) -> p a i m", i=PACK),
-        )
+        v_words.append(placed("v_words1", [P, S], U32, 61440))
+        nc.vector.tensor_copy(v_words[1][:], tab[1][:].indirect(pick[:]))
+        load_soil(placed("soil1", [P, S], F32, 4 * T + 4 * S))
+        w2_planes = placed("w2_planes", [P, PASSES, H], U8, 4 * T)
         nc.vector.tensor_copy(
             out=w2_planes[:].rearrange("p a (i m) -> p a i m", i=PACK),
             in_=w2_planes_raw[:].rearrange("p a (m i) -> p a i m", i=PACK),
         )
-
-        nc.vector.tensor_copy(v_words[1][:], tab[1][:].indirect(pick[:]))
-        load_soil(placed("soil1", [P, S], F32, 4 * T + 4 * S))
 
         w1_codes = {}
         w1_planes = {}
@@ -227,20 +231,19 @@ def tile_list_needle_loss_plans_kernel(
         load_soil(placed("soil2", [P, S], F32, 8 * T))
         load_soil(placed("soil3", [P, S], F32, 8 * T + 4 * S))
         quantise_w1(0, 1, PACK, placed("w1_bf0_rest", [P, PACK - 1, P, PACK], BF16, MID + 3072))
-        w3_raw = held("w3_raw", [P, PACK, N], F32, tag="w1_raw0")
+        w3_raw = placed("w3_raw", [P, PACK, N], F32, 12 * T)
         nc.sync.dma_start(out=w3_raw[:], in_=w3.rearrange("(p j) n -> p j n", j=PACK))
         late_page(placed("page1", [P, T2], F32, MID + 1024 - 4 * T2))
         late_page(placed("page2", [P, T2], F32, MID + 5120))
         h = placed("h0_second", [P, BANK], F32, MID + 2048)
         weigh(0, [h[:]], sums[1:])
-        wgt_sb = held("wgt_sb", [P, PICKS], F32, tag="soil0")
+        wgt_sb = placed("wgt_sb", [P, PICKS], F32, 4 * S)
         nc.sync.dma_start(out=wgt_sb[:], in_=wgt)
         add([h[:]], sums[1:])
         scatter_half(1, h)
         sums = products(1)
         h = placed("h1", [P, S], F32, MID + 1024)
         weigh(1, halves(h), sums)
-        late_page(placed("page3", [P, T2], F32, 4 * T))
         add(halves(h), sums)
         for i in range(1, PACK - 1):
             sums = products(i + 1)
@@ -251,6 +254,7 @@ def tile_list_needle_loss_plans_kernel(
             h = ahead
         frost_sb = held("frost_sb", [P, PACK, PICKS], F32, tag="v_words0")
         nc.sync.dma_start(out=frost_sb[:], in_=frost.rearrange("(p i) m -> p i m", i=PACK))
+        late_page(placed("page3", [P, T2], F32, 4 * T))
         quantise_w3()
         scatter(PACK - 1, h)
 
@@ -263,7 +267,7 @@ def tile_list_needle_loss_plans_kernel(
         def gather(c, i):
             m0, width = starts[c], CHUNKS[c]
             if i == 0:
-                gap[c] = ring.tile([P, PACK, width], F32, name="gap")
+                gap[c] = held("gap%d" % c, [P, PACK, width], F32, tag="gap_slot%d" % GAP_SLOT[c])
             nc.vector.tensor_tensor(
                 gap[c][:, i, :],
                 pages[i][:].indirect(read[:, m0 // 16 : (m0 + width) // 16]),
@@ -278,8 +282,8 @@ def tile_list_needle_loss_plans_kernel(
         def clip(c):
             width = CHUNKS[c]
             rounded_z[c] = held("z_bf%d" % c, [P, width, PACK], BF16)
-            dst = rounded_z[c][:].rearrange("p (g k) i -> p g i k", k=4)
-            src = gap[c][:].rearrange("p i (g k) -> p g i k", k=4)
+            dst = rounded_z[c][:]
+            src = gap[c][:].rearrange("p i m -> p m i")
             if c in RELU_ON_VECTOR:
                 nc.vector.tensor_scalar_max(dst, src, 0.0)
             else:
@@ -293,6 +297,7 @@ def tile_list_needle_loss_plans_kernel(
                 out=codes[:].bitcast(FP8X4), scales=plane[:], in_=rounded_z[c][:].rearrange("p m i -> p (m i)")
             )
             per_bank = 2 if width == 256 else 3
+            sizes = []
             for t0 in range(0, N_TILES, per_bank):
                 acc = bank(banks_used[0])
                 banks_used[0] = banks_used[0] + 1
@@ -306,9 +311,11 @@ def tile_list_needle_loss_plans_kernel(
                         start=True,
                         stop=True,
                     )
-                size = ring.tile([P, per_bank * width], F32, name="size", bufs=3)
-                result = ring.tile([P, per_bank, width], F32, name="result", bufs=4)
+                size = ring.tile([P, per_bank * width], F32, name="size", bufs=6)
                 nc.scalar.activation(size[:], acc[:, : per_bank * width], ACT.Abs)
+                sizes.append((t0, size))
+            for t0, size in sizes:
+                result = held("result%d_%d" % (c, t0), [P, per_bank, width], F32)
                 nc.scalar.activation(result[:].rearrange("p t m -> p (t m)"), size[:], ACT.Ln, bias=1.0)
                 nc.sync.dma_start(out=out_rows[:, t0 : t0 + per_bank, m0 : m0 + width], in_=result[:])
 

@@ -1,6 +1,7 @@
 from contextlib import ExitStack
 
 import concourse.mybir as mybir
+from concourse.masks import make_identity
 
 K, T, S, PICKS, T2, H, N = 1024, 2048, 1024, 1024, 2048, 512, 768
 FLOPS = 2 * (2 * K * H * S + H * N * PICKS)
@@ -22,8 +23,8 @@ PASSES = K // (P * PACK)
 BANK = 512
 HALVES = S // BANK
 N_TILES = N // P
-CHUNKS = (128, 256, 256, 128, 128, 128)
-GAP_SLOT = (0, 0, 1, 0, 1, 1)
+CHUNKS = (128, 256, 256, 256, 128)
+LATE_SLOT = (0, 0, 1, 0, 0)
 MID = 44032
 RELU_ON_VECTOR = (0, 1, 2, 3, 4, 5)
 
@@ -55,13 +56,14 @@ def tile_list_needle_loss_plans_kernel(
         tab_planes = placed("tab_planes", [P, T], U8, 60416)
         w2_planes_raw = held("w2_planes_raw", [P, PASSES, H], U8)
         v_plane_low = held("v_plane_low", [P, S], U8)
-        pages = [held("page0", [P, T2], F32)]
+        pages = [held("page%d" % n, [P, T2], F32) for n in range(3)]
         nc.vector.memset(tab_planes[:].bitcast(U32), 0)
         nc.gpsimd.memset(w2_planes_raw[:].rearrange("p a c -> p (a c)").bitcast(U32), 0)
         nc.vector.memset(v_plane_low[:].bitcast(U32), 0)
-        for page in pages:
-            nc.vector.memset(page[:, : T2 // 2 - 1], 0.0)
-            nc.vector.memset(page[:, T2 // 2 - 1 :], 0.0)
+        nc.vector.memset(pages[0][:, : T2 // 2 - 1], 0.0)
+        nc.vector.memset(pages[0][:, T2 // 2 - 1 :], 0.0)
+        nc.vector.memset(pages[1][:], 0.0)
+        nc.vector.memset(pages[2][:], 0.0)
 
         tab = [placed("tab%d" % a, [P, T], U32, 4 * T * a) for a in range(PASSES)]
         w1_raw = []
@@ -101,6 +103,8 @@ def tile_list_needle_loss_plans_kernel(
                 in_=w2_scales[:, 4 * q : 4 * q + 4, :].rearrange("a r c -> r a c").bitcast(I32),
             )
 
+        identity = held("identity", [P, P], F32)
+        make_identity(nc, identity[:])
         w2_codes = held("w2_codes", [P, PASSES, 2 * H], U8)
         nc.scalar.copy(
             out=w2_codes[:].bitcast(U16).rearrange("p a (i m) -> p a i m", i=PACK),
@@ -156,7 +160,8 @@ def tile_list_needle_loss_plans_kernel(
             sums = []
             for half in range(HALVES):
                 cols = slice(half * BANK, (half + 1) * BANK)
-                sums.append((cols, bank(4 * i + 2 * half), bank(4 * i + 2 * half + 1)))
+                base = 4 if i == 1 else 0
+                sums.append((cols, bank(base + 2 * half), bank(base + 2 * half + 1)))
             for a in range(PASSES):
                 for cols, first, second in sums:
                     nc.tensor.matmul_mx(
@@ -192,7 +197,7 @@ def tile_list_needle_loss_plans_kernel(
             return [h[:, half * BANK : (half + 1) * BANK] for half in range(HALVES)]
 
         def scatter(i, h):
-            nc.vector.tensor_tensor(pages[i][:].indirect(put[:]), h[:], wgs_sb[:], ALU.mult)
+            nc.vector.tensor_tensor(pages[i % 3][:].indirect(put[:]), h[:], wgs_sb[:], ALU.mult)
 
         def scatter_half(half, h):
             nc.vector.tensor_tensor(
@@ -207,20 +212,13 @@ def tile_list_needle_loss_plans_kernel(
 
         def quantise_w3():
             rounded = held("w3_bf", [P, N, PACK], BF16)
-            nc.scalar.copy(
-                out=rounded[:].rearrange("p (c k) j -> p c j k", k=4),
-                in_=w3_raw[:].rearrange("p j (c k) -> p c j k", k=4),
-            )
+            nc.scalar.copy(out=rounded[:], in_=w3_raw[:].rearrange("p j n -> p n j"))
             for n0, n1 in ((0, 512), (512, N)):
                 nc.vector.quantize_mx(
                     out=w3_codes[:, n0:n1].bitcast(FP8X4),
                     scales=w3_plane[:, n0:n1],
                     in_=rounded[:, n0:n1, :].rearrange("p n j -> p (n j)"),
                 )
-
-        def late_page(page):
-            nc.gpsimd.memset(page[:], 0.0)
-            pages.append(page)
 
         sums = products(0)
         h = held("h0_first", [P, BANK], F32)
@@ -233,74 +231,89 @@ def tile_list_needle_loss_plans_kernel(
         quantise_w1(0, 1, PACK, placed("w1_bf0_rest", [P, PACK - 1, P, PACK], BF16, MID + 3072))
         w3_raw = placed("w3_raw", [P, PACK, N], F32, 12 * T)
         nc.sync.dma_start(out=w3_raw[:], in_=w3.rearrange("(p j) n -> p j n", j=PACK))
-        late_page(placed("page1", [P, T2], F32, MID + 1024 - 4 * T2))
-        late_page(placed("page2", [P, T2], F32, MID + 5120))
         h = placed("h0_second", [P, BANK], F32, MID + 2048)
         weigh(0, [h[:]], sums[1:])
         wgt_sb = placed("wgt_sb", [P, PICKS], F32, 4 * S)
         nc.sync.dma_start(out=wgt_sb[:], in_=wgt)
+        frost_sb = held("frost_sb", [P, PACK, PICKS], F32, tag="h0_first")
+        nc.sync.dma_start(out=frost_sb[:], in_=frost.rearrange("(p i) m -> p i m", i=PACK))
         add([h[:]], sums[1:])
         scatter_half(1, h)
         sums = products(1)
         h = placed("h1", [P, S], F32, MID + 1024)
         weigh(1, halves(h), sums)
         add(halves(h), sums)
-        for i in range(1, PACK - 1):
-            sums = products(i + 1)
-            ahead = held("h2", [P, S], F32) if i == 1 else placed("h3", [P, S], F32, MID + 1024)
-            weigh(i + 1, halves(ahead), sums)
-            scatter(i, h)
-            add(halves(ahead), sums)
-            h = ahead
-        frost_sb = held("frost_sb", [P, PACK, PICKS], F32, tag="v_words0")
-        nc.sync.dma_start(out=frost_sb[:], in_=frost.rearrange("(p i) m -> p i m", i=PACK))
-        late_page(placed("page3", [P, T2], F32, 4 * T))
-        quantise_w3()
-        scatter(PACK - 1, h)
-
         starts = [sum(CHUNKS[:c]) for c in range(len(CHUNKS))]
         out_rows = out.rearrange("(t p) m -> p t m", p=P)
-        gap = {}
-        rounded_z = {}
-        banks_used = [0]
+        gap = held("gap", [P, PACK, PICKS], F32)
 
-        def gather(c, i):
+        def gather(c, i, dst):
             m0, width = starts[c], CHUNKS[c]
-            if i == 0:
-                gap[c] = held("gap%d" % c, [P, PACK, width], F32, tag="gap_slot%d" % GAP_SLOT[c])
             nc.vector.tensor_tensor(
-                gap[c][:, i, :],
-                pages[i][:].indirect(read[:, m0 // 16 : (m0 + width) // 16]),
+                dst,
+                pages[i % 3][:].indirect(read[:, m0 // 16 : (m0 + width) // 16]),
                 wgt_sb[:, m0 : m0 + width],
                 ALU.mult,
             )
 
-        def subtract(c):
-            m0, width = starts[c], CHUNKS[c]
-            nc.vector.tensor_tensor(gap[c][:], frost_sb[:, :, m0 : m0 + width], gap[c][:], ALU.subtract)
+        def add_on_tensor(i, weighed, sums):
+            h = held("h%d" % i, [P, S], F32)
+            for half, (cols, first, second) in enumerate(sums):
+                plain = ring.tile([P, BANK], F32, name="plain")
+                nc.scalar.copy(plain[:], second[:])
+                turned = bank(4 + half)
+                for b0 in range(0, BANK, P):
+                    block = slice(b0, b0 + P)
+                    nc.tensor.matmul(
+                        turned[:, block], weighed[half][:, block], identity[:], start=True, stop=False, is_transpose=True
+                    )
+                    nc.tensor.matmul(
+                        turned[:, block], plain[:, block], identity[:], start=False, stop=True, is_transpose=True
+                    )
+                turned_sb = ring.tile([P, BANK], F32, name="turned_sb")
+                nc.scalar.copy(turned_sb[:], turned[:])
+                back = bank(6 + half)
+                for b0 in range(0, BANK, P):
+                    block = slice(b0, b0 + P)
+                    nc.tensor.transpose(back[:, block], turned_sb[:, block], identity[:])
+                nc.scalar.copy(h[:, cols], back[:])
+            return h
 
-        def clip(c):
-            width = CHUNKS[c]
-            rounded_z[c] = held("z_bf%d" % c, [P, width, PACK], BF16)
-            dst = rounded_z[c][:]
-            src = gap[c][:].rearrange("p i m -> p m i")
-            if c in RELU_ON_VECTOR:
-                nc.vector.tensor_scalar_max(dst, src, 0.0)
-            else:
-                nc.scalar.activation(dst, src, ACT.Relu)
+        sums = products(2)
+        weighed = halves(held("weighed2", [P, S], F32))
+        weigh(2, weighed, sums)
+        h2 = add_on_tensor(2, weighed, sums)
+        scatter(1, h)
+        nc.vector.tensor_tensor(gap[:, 0, :], pages[0][:].indirect(read[:]), wgt_sb[:], ALU.mult)
+        sums = products(3)
+        weighed = halves(placed("weighed3", [P, S], F32, MID + 1024))
+        weigh(3, weighed, sums)
+        h3 = add_on_tensor(3, weighed, sums)
+        scatter(2, h2)
+        nc.vector.tensor_tensor(gap[:, 0, :], frost_sb[:, 0, :], gap[:, 0, :], ALU.subtract)
+        quantise_w3()
+        scatter(3, h3)
 
-        def finish(c):
-            m0, width = starts[c], CHUNKS[c]
+        banks_used = 0
+        for c, width in enumerate(CHUNKS):
+            m0 = starts[c]
+            late = held("late%d" % c, [P, PACK - 1, width], F32, tag="late_slot%d" % LATE_SLOT[c])
+            for i in range(1, PACK):
+                gather(c, i, late[:, i - 1, :])
+            cols = slice(m0, m0 + width)
+            nc.vector.tensor_tensor(gap[:, 1:, cols], frost_sb[:, 1:, cols], late[:], ALU.subtract)
+            rounded = held("z_bf%d" % c, [P, width, PACK], BF16, tag="late_slot1" if c == 0 else None)
+            nc.vector.tensor_scalar_max(rounded[:], gap[:, :, cols].rearrange("p i m -> p m i"), 0.0)
             codes = held("z_codes%d" % c, [P, width], U32)
             plane = held("z_plane%d" % c, [P, width], U8)
             nc.vector.quantize_mx(
-                out=codes[:].bitcast(FP8X4), scales=plane[:], in_=rounded_z[c][:].rearrange("p m i -> p (m i)")
+                out=codes[:].bitcast(FP8X4), scales=plane[:], in_=rounded[:].rearrange("p m i -> p (m i)")
             )
             per_bank = 2 if width == 256 else 3
             sizes = []
             for t0 in range(0, N_TILES, per_bank):
-                acc = bank(banks_used[0])
-                banks_used[0] = banks_used[0] + 1
+                acc = bank(banks_used)
+                banks_used = banks_used + 1
                 for t in range(t0, t0 + per_bank):
                     nc.tensor.matmul_mx(
                         out=acc[:, (t - t0) * width : (t - t0 + 1) * width],
@@ -318,10 +331,3 @@ def tile_list_needle_loss_plans_kernel(
                 result = held("result%d_%d" % (c, t0), [P, per_bank, width], F32)
                 nc.scalar.activation(result[:].rearrange("p t m -> p (t m)"), size[:], ACT.Ln, bias=1.0)
                 nc.sync.dma_start(out=out_rows[:, t0 : t0 + per_bank, m0 : m0 + width], in_=result[:])
-
-        for c in range(len(CHUNKS)):
-            for i in range(PACK):
-                gather(c, i)
-            subtract(c)
-            clip(c)
-            finish(c)

from contextlib import ExitStack

import concourse.mybir as mybir
from concourse.masks import make_identity

K, T, S, PICKS, T2, H, N = 1024, 2048, 1024, 1024, 2048, 512, 768
FLOPS = 2 * (2 * K * H * S + H * N * PICKS)

F32 = mybir.dt.float32
BF16 = mybir.dt.bfloat16
I32 = mybir.dt.int32
U32 = mybir.dt.uint32
U16 = mybir.dt.uint16
U8 = mybir.dt.uint8
FP8X4 = mybir.dt.float8_e4m3fn_x4
FP4X4 = mybir.dt.float4_e2m1fn_x4
ALU = mybir.AluOpType
ACT = mybir.ActivationFunctionType

P = 128
PACK = 4
PASSES = K // (P * PACK)
BANK = 512
HALVES = S // BANK
N_TILES = N // P
CHUNKS = (128, 256, 256, 256, 128)
LATE_SLOT = (0, 0, 1, 0, 0)
MID = 44032
RELU_ON_VECTOR = (0, 1, 2, 3, 4, 5)


def tile_list_needle_loss_plans_kernel(
    tc, tab_words, tab_scales, offs, offs2, offs3, w1, w2_words, w2_scales, soil, wgs, wgt, frost, w3, out
):
    nc = tc.nc
    with ExitStack() as ctx:
        lists = ctx.enter_context(tc.tile_pool(name="lists", bufs=1))
        keep = ctx.enter_context(tc.tile_pool(name="keep", bufs=1))
        ring = ctx.enter_context(tc.tile_pool(name="ring", bufs=2))
        arena = ctx.enter_context(tc.tile_pool(name="arena", bufs=1))
        psum = ctx.enter_context(tc.psum_pool(name="psum", bufs=1))

        def held(name, shape, dtype, tag=None):
            return keep.tile(shape, dtype, name=name, tag=tag or name, align_bytes=64)

        def placed(name, shape, dtype, offset):
            return arena.tile(shape, dtype, name=name, align_bytes=64, offset=offset)

        def bank(index):
            return psum.tile([P, BANK], F32, name="bank%d" % (index % 8), tag="bank%d" % (index % 8))

        pick = lists.tile([P, S // 16], U16, name="pick")
        put = lists.tile([P, S // 16], U16, name="put")
        read = lists.tile([P, PICKS // 16], U16, name="read")

        tab_planes = placed("tab_planes", [P, T], U8, 60416)
        w2_planes_raw = held("w2_planes_raw", [P, PASSES, H], U8)
        v_plane_low = held("v_plane_low", [P, S], U8)
        pages = [held("page%d" % n, [P, T2], F32) for n in range(3)]
        nc.vector.memset(tab_planes[:].bitcast(U32), 0)
        nc.gpsimd.memset(w2_planes_raw[:].rearrange("p a c -> p (a c)").bitcast(U32), 0)
        nc.vector.memset(v_plane_low[:].bitcast(U32), 0)
        nc.vector.memset(pages[0][:, : T2 // 2 - 1], 0.0)
        nc.vector.memset(pages[0][:, T2 // 2 - 1 :], 0.0)
        nc.vector.memset(pages[1][:], 0.0)
        nc.vector.memset(pages[2][:], 0.0)

        tab = [placed("tab%d" % a, [P, T], U32, 4 * T * a) for a in range(PASSES)]
        w1_raw = []
        w2_raw = placed("w2_raw", [P, PASSES, 2 * H], U8, 12 * T - 2 * H)
        soil_rows = soil.rearrange("(p i) j -> i p j", i=PACK)
        soil_sb = []

        def load_tab(a):
            nc.sync.dma_start(
                out=tab[a][:].bitcast(I32), in_=tab_words[a].rearrange("p t i -> p (t i)").bitcast(I32)
            )

        def load_w1(a):
            w1_raw.append(placed("w1_raw%d" % a, [P, PACK, H], F32, 12 * T - 4 * T * a))
            nc.sync.dma_start(
                out=w1_raw[a][:], in_=w1[512 * a : 512 * (a + 1), :].rearrange("(p j) c -> p j c", j=PACK)
            )

        def load_soil(tile):
            nc.sync.dma_start(out=tile[:], in_=soil_rows[len(soil_sb)])
            soil_sb.append(tile)

        nc.sync.dma_start(pick[:], offs)
        nc.sync.dma_start(put[:], offs2)
        nc.sync.dma_start(read[:], offs3)
        nc.sync.dma_start(out=w2_raw[:].bitcast(I32), in_=w2_words.rearrange("a p c -> p a c").bitcast(I32))
        load_tab(0)
        load_tab(1)
        for q in range(4):
            nc.sync.dma_start(
                out=tab_planes[32 * q : 32 * q + 4 * PASSES, :].bitcast(I32),
                in_=tab_scales[:, 4 * q : 4 * q + 4, :].bitcast(I32),
            )
        for q in range(4):
            nc.gpsimd.dma_start(
                out=w2_planes_raw[32 * q : 32 * q + 4, :, :].bitcast(I32),
                in_=w2_scales[:, 4 * q : 4 * q + 4, :].rearrange("a r c -> r a c").bitcast(I32),
            )

        identity = held("identity", [P, P], F32)
        make_identity(nc, identity[:])
        w2_codes = held("w2_codes", [P, PASSES, 2 * H], U8)
        nc.scalar.copy(
            out=w2_codes[:].bitcast(U16).rearrange("p a (i m) -> p a i m", i=PACK),
            in_=w2_raw[:].bitcast(U16).rearrange("p a (m i) -> p a i m", i=PACK),
        )
        load_w1(0)
        load_w1(1)

        v_words = [held("v_words0", [P, S], U32)]
        nc.vector.tensor_copy(v_words[0][:], tab[0][:].indirect(pick[:]))
        load_soil(placed("soil0", [P, S], F32, 4 * S))
        v_planes = placed("v_planes", [P, S], U8, 0)
        nc.vector.tensor_copy(v_planes[:], tab_planes[:].indirect(pick[:]))
        for q in range(4):
            nc.sync.dma_start(
                out=v_plane_low[32 * q : 32 * q + 4, :].bitcast(I32),
                in_=v_planes[32 * q + 4 : 32 * q + 8, :].bitcast(I32),
            )
        wgs_sb = placed("wgs_sb", [P, S], F32, 57344)
        nc.sync.dma_start(out=wgs_sb[:], in_=wgs)

        v_words.append(placed("v_words1", [P, S], U32, 61440))
        nc.vector.tensor_copy(v_words[1][:], tab[1][:].indirect(pick[:]))
        load_soil(placed("soil1", [P, S], F32, 4 * T + 4 * S))
        w2_planes = placed("w2_planes", [P, PASSES, H], U8, 4 * T)
        nc.vector.tensor_copy(
            out=w2_planes[:].rearrange("p a (i m) -> p a i m", i=PACK),
            in_=w2_planes_raw[:].rearrange("p a (m i) -> p a i m", i=PACK),
        )

        w1_codes = {}
        w1_planes = {}

        def quantise_w1(a, i0, i1, rounded):
            count = i1 - i0
            codes = held("w1_codes%d_%d" % (a, i0), [P, count * P], U32)
            plane = held("w1_plane%d_%d" % (a, i0), [P, count * P], U8)
            nc.scalar.copy(
                out=rounded[:].rearrange("p i m j -> p m i j"),
                in_=w1_raw[a][:].rearrange("p j (m i) -> p m i j", i=PACK)[:, :, i0:i1, :],
            )
            nc.vector.quantize_mx(
                out=codes[:].bitcast(FP8X4), scales=plane[:], in_=rounded[:].rearrange("p i m j -> p (i m j)")
            )
            for i in range(i0, i1):
                w1_codes[a, i] = codes[:, (i - i0) * P : (i - i0 + 1) * P]
                w1_planes[a, i] = plane[:, (i - i0) * P : (i - i0 + 1) * P]

        quantise_w1(0, 0, 1, held("w1_bf0", [P, 1, P, PACK], BF16))
        quantise_w1(1, 0, 1, placed("w1_bf1", [P, 1, P, PACK], BF16, MID + 4096))

        def products(i):
            sums = []
            for half in range(HALVES):
                cols = slice(half * BANK, (half + 1) * BANK)
                base = 4 if i == 1 else 0
                sums.append((cols, bank(base + 2 * half), bank(base + 2 * half + 1)))
            for a in range(PASSES):
                for cols, first, second in sums:
                    nc.tensor.matmul_mx(
                        out=second[:],
                        lhsT=w2_codes[:, a, 2 * i * P : 2 * (i + 1) * P].bitcast(FP4X4),
                        lhsT_scale=w2_planes[:, a, i * P : (i + 1) * P],
                        rhs=v_words[a][:, cols].bitcast(FP8X4),
                        rhs_scale=v_planes[:, cols] if a == 0 else v_plane_low[:, cols],
                        start=(a == 0),
                        stop=(a == PASSES - 1),
                    )
                for cols, first, second in sums:
                    nc.tensor.matmul_mx(
                        out=first[:],
                        lhsT=w1_codes[a, i].bitcast(FP8X4),
                        lhsT_scale=w1_planes[a, i],
                        rhs=v_words[a][:, cols].bitcast(FP8X4),
                        rhs_scale=v_planes[4 * a : P, cols],
                        start=(a == 0),
                        stop=(a == PASSES - 1),
                    )
            return sums

        def weigh(i, h, sums):
            for part, (cols, first, second) in zip(h, sums):
                nc.vector.tensor_tensor(part, first[:], soil_sb[i][:, cols], ALU.mult)

        def add(h, sums):
            for part, (cols, first, second) in zip(h, sums):
                nc.vector.tensor_tensor(part, second[:], part, ALU.add)

        def halves(h):
            return [h[:, half * BANK : (half + 1) * BANK] for half in range(HALVES)]

        def scatter(i, h):
            nc.vector.tensor_tensor(pages[i % 3][:].indirect(put[:]), h[:], wgs_sb[:], ALU.mult)

        def scatter_half(half, h):
            nc.vector.tensor_tensor(
                pages[0][:].indirect(put[:, half * BANK // 16 : (half + 1) * BANK // 16]),
                h[:],
                wgs_sb[:, half * BANK : (half + 1) * BANK],
                ALU.mult,
            )

        w3_codes = held("w3_codes", [P, N], U32)
        w3_plane = held("w3_plane", [P, N], U8)

        def quantise_w3():
            rounded = held("w3_bf", [P, N, PACK], BF16)
            nc.scalar.copy(out=rounded[:], in_=w3_raw[:].rearrange("p j n -> p n j"))
            for n0, n1 in ((0, 512), (512, N)):
                nc.vector.quantize_mx(
                    out=w3_codes[:, n0:n1].bitcast(FP8X4),
                    scales=w3_plane[:, n0:n1],
                    in_=rounded[:, n0:n1, :].rearrange("p n j -> p (n j)"),
                )

        sums = products(0)
        h = held("h0_first", [P, BANK], F32)
        weigh(0, [h[:]], sums[:1])
        add([h[:]], sums[:1])
        scatter_half(0, h)
        quantise_w1(1, 1, PACK, placed("w1_bf1_rest", [P, PACK - 1, P, PACK], BF16, MID))
        load_soil(placed("soil2", [P, S], F32, 8 * T))
        load_soil(placed("soil3", [P, S], F32, 8 * T + 4 * S))
        quantise_w1(0, 1, PACK, placed("w1_bf0_rest", [P, PACK - 1, P, PACK], BF16, MID + 3072))
        w3_raw = placed("w3_raw", [P, PACK, N], F32, 12 * T)
        nc.sync.dma_start(out=w3_raw[:], in_=w3.rearrange("(p j) n -> p j n", j=PACK))
        h = placed("h0_second", [P, BANK], F32, MID + 2048)
        weigh(0, [h[:]], sums[1:])
        wgt_sb = placed("wgt_sb", [P, PICKS], F32, 4 * S)
        nc.sync.dma_start(out=wgt_sb[:], in_=wgt)
        frost_sb = held("frost_sb", [P, PACK, PICKS], F32, tag="h0_first")
        nc.sync.dma_start(out=frost_sb[:], in_=frost.rearrange("(p i) m -> p i m", i=PACK))
        add([h[:]], sums[1:])
        scatter_half(1, h)
        sums = products(1)
        h = placed("h1", [P, S], F32, MID + 1024)
        weigh(1, halves(h), sums)
        add(halves(h), sums)
        starts = [sum(CHUNKS[:c]) for c in range(len(CHUNKS))]
        out_rows = out.rearrange("(t p) m -> p t m", p=P)
        gap = held("gap", [P, PACK, PICKS], F32)

        def gather(c, i, dst):
            m0, width = starts[c], CHUNKS[c]
            nc.vector.tensor_tensor(
                dst,
                pages[i % 3][:].indirect(read[:, m0 // 16 : (m0 + width) // 16]),
                wgt_sb[:, m0 : m0 + width],
                ALU.mult,
            )

        def add_on_tensor(i, weighed, sums):
            h = held("h%d" % i, [P, S], F32)
            for half, (cols, first, second) in enumerate(sums):
                plain = ring.tile([P, BANK], F32, name="plain")
                nc.scalar.copy(plain[:], second[:])
                turned = bank(4 + half)
                for b0 in range(0, BANK, P):
                    block = slice(b0, b0 + P)
                    nc.tensor.matmul(
                        turned[:, block], weighed[half][:, block], identity[:], start=True, stop=False, is_transpose=True
                    )
                    nc.tensor.matmul(
                        turned[:, block], plain[:, block], identity[:], start=False, stop=True, is_transpose=True
                    )
                turned_sb = ring.tile([P, BANK], F32, name="turned_sb")
                nc.scalar.copy(turned_sb[:], turned[:])
                back = bank(6 + half)
                for b0 in range(0, BANK, P):
                    block = slice(b0, b0 + P)
                    nc.tensor.transpose(back[:, block], turned_sb[:, block], identity[:])
                nc.scalar.copy(h[:, cols], back[:])
            return h

        sums = products(2)
        weighed = halves(held("weighed2", [P, S], F32))
        weigh(2, weighed, sums)
        h2 = add_on_tensor(2, weighed, sums)
        scatter(1, h)
        nc.vector.tensor_tensor(gap[:, 0, :], pages[0][:].indirect(read[:]), wgt_sb[:], ALU.mult)
        sums = products(3)
        weighed = halves(placed("weighed3", [P, S], F32, MID + 1024))
        weigh(3, weighed, sums)
        h3 = add_on_tensor(3, weighed, sums)
        scatter(2, h2)
        nc.vector.tensor_tensor(gap[:, 0, :], frost_sb[:, 0, :], gap[:, 0, :], ALU.subtract)
        quantise_w3()
        scatter(3, h3)

        banks_used = 0
        for c, width in enumerate(CHUNKS):
            m0 = starts[c]
            late = held("late%d" % c, [P, PACK - 1, width], F32, tag="late_slot%d" % LATE_SLOT[c])
            for i in range(1, PACK):
                gather(c, i, late[:, i - 1, :])
            cols = slice(m0, m0 + width)
            nc.vector.tensor_tensor(gap[:, 1:, cols], frost_sb[:, 1:, cols], late[:], ALU.subtract)
            rounded = held("z_bf%d" % c, [P, width, PACK], BF16, tag="late_slot1" if c == 0 else None)
            nc.vector.tensor_scalar_max(rounded[:], gap[:, :, cols].rearrange("p i m -> p m i"), 0.0)
            codes = held("z_codes%d" % c, [P, width], U32)
            plane = held("z_plane%d" % c, [P, width], U8)
            nc.vector.quantize_mx(
                out=codes[:].bitcast(FP8X4), scales=plane[:], in_=rounded[:].rearrange("p m i -> p (m i)")
            )
            per_bank = 2 if width == 256 else 3
            sizes = []
            for t0 in range(0, N_TILES, per_bank):
                acc = bank(banks_used)
                banks_used = banks_used + 1
                for t in range(t0, t0 + per_bank):
                    nc.tensor.matmul_mx(
                        out=acc[:, (t - t0) * width : (t - t0 + 1) * width],
                        lhsT=w3_codes[:, t * P : (t + 1) * P].bitcast(FP8X4),
                        lhsT_scale=w3_plane[:, t * P : (t + 1) * P],
                        rhs=codes[:].bitcast(FP8X4),
                        rhs_scale=plane[:],
                        start=True,
                        stop=True,
                    )
                size = ring.tile([P, per_bank * width], F32, name="size", bufs=6)
                nc.scalar.activation(size[:], acc[:, : per_bank * width], ACT.Abs)
                sizes.append((t0, size))
            for t0, size in sizes:
                result = held("result%d_%d" % (c, t0), [P, per_bank, width], F32)
                nc.scalar.activation(result[:].rearrange("p t m -> p (t m)"), size[:], ACT.Ln, bias=1.0)
                nc.sync.dma_start(out=out_rows[:, t0 : t0 + per_bank, m0 : m0 + width], in_=result[:])
